import numpy as np
import ml_dtypes


def mxq(x, axis, fmt="e4m3"):
    dtype, down = {"e4m3": (ml_dtypes.float8_e4m3fn, 7), "e5m2": (ml_dtypes.float8_e5m2, 14)}[fmt]
    v = np.moveaxis(np.asarray(x, np.float32).astype(ml_dtypes.bfloat16).astype(np.float64), axis, -1)
    blocks = v.reshape(v.shape[:-1] + (-1, 32))
    amax = np.abs(blocks).max(-1, keepdims=True)
    byte = np.maximum(np.where(amax > 0, np.frexp(amax)[1] - 1 + 127, 0) - down, 1)
    scale = np.exp2(byte - 127.0)
    codes = (blocks / scale).astype(np.float32).astype(dtype).astype(np.float64)
    return np.moveaxis((codes * scale).reshape(v.shape), -1, axis)


WIDE = False


def mx_kscale(k):
    if not WIDE:
        return np.ones(k)
    levels = np.array([10, -10, 5, -5, 0])
    if k % 512:
        return np.exp2(np.random.permutation(np.resize(levels, k // 32))).repeat(32)
    a = np.empty((k // 512, 16))
    for p in range(k // 512):
        a[p, :8] = np.random.permutation(np.resize(levels, 8))
        for g in range(8):
            far = levels[np.abs(levels - a[p, g]) >= 10]
            a[p, g + 8] = far[np.random.randint(len(far))]
    return np.exp2(a.ravel()).repeat(32)


def f64(x):
    return np.asarray(x).astype(np.float64)


def striped(idx):
    return np.tile(np.asarray(idx).reshape(-1, 16).T, (8, 1)).astype(np.uint16)


def unstriped(offs):
    return offs[:16].T.reshape(-1).astype(np.int64)


E2M1 = np.array([0.0, 0.5, 1.0, 1.5, 2.0, 3.0, 4.0, 6.0, -0.0, -0.5, -1.0, -1.5, -2.0, -3.0, -4.0, -6.0])


def pack_weight(w, fmt):
    k, n = w.shape
    w = f64(np.asarray(w, np.float32).astype(ml_dtypes.bfloat16)).reshape(k // 32, 32, n)
    amax = np.abs(w).max(1)
    if fmt == "e4m3":
        byte = np.frexp(amax)[1] - 1 + 127 - 7
    else:
        mant, ex = np.frexp(amax / 6.0)
        byte = np.where(mant > 0.5, ex, ex - 1) + 127
    byte = np.clip(np.where(amax > 0, byte, 1), 1, 254)
    scaled = (w * np.exp2(127.0 - byte)[:, None, :]).reshape(k, n).astype(np.float32)
    by_word = np.ascontiguousarray(scaled.reshape(k // 512, 128, 4, n).transpose(0, 1, 3, 2))
    if fmt == "e4m3":
        words = by_word.astype(ml_dtypes.float8_e4m3fn).view(np.uint8)
    else:
        c = by_word.astype(ml_dtypes.float4_e2m1fn).view(np.uint8) & 0xF
        words = (c[..., 0::2] | (c[..., 1::2] << 4)).reshape(k // 512, 128, 2 * n)
    return np.ascontiguousarray(words), np.ascontiguousarray(byte.astype(np.uint8).reshape(k // 512, 16, n))


def unpack_weight(words, scales, fmt):
    g, _, n = scales.shape
    words = np.ascontiguousarray(words).reshape(g, 128, n, -1)
    if fmt == "e4m3":
        vals = words.view(ml_dtypes.float8_e4m3fn).astype(np.float64)
    else:
        nib = np.empty((g, 128, n, 4), np.uint8)
        nib[..., 0::2] = words & 0xF
        nib[..., 1::2] = words >> 4
        vals = E2M1[nib]
    vals = vals * np.repeat(np.exp2(scales.astype(np.float64) - 127.0), 8, axis=1)[..., None]
    return vals.transpose(0, 1, 3, 2).reshape(g * 512, n)


def bf(x):
    return np.asarray(x, np.float32).astype(ml_dtypes.bfloat16)


def planes(Y):
    r, m = Y.shape
    b = f64(bf(Y)).reshape(r // 32, 32, m)
    amax = np.abs(b).max(1)
    byte = np.clip(np.where(amax > 0, np.frexp(amax)[1] - 1 + 127 - 7, 1), 1, 254)
    codes = (b * np.exp2(127.0 - byte)[:, None, :]).reshape(r, m).astype(np.float32).astype(ml_dtypes.float8_e4m3fn).view(np.uint8)
    words = codes.reshape(r // 512, 128, 4, m).transpose(0, 1, 3, 2)
    return np.ascontiguousarray(words), np.ascontiguousarray(byte.astype(np.uint8).reshape(r // 512, 16, m))


D, T, I, Q = 512, 1024, 512, 256


def setup_inputs():
    n = np.random.standard_normal
    idx = np.random.permutation(T)[:I]
    fi = mx_kscale(I)
    fd = mx_kscale(D)
    ti = np.ones(T)
    ti[idx] = fi
    atomp = pack_weight(n((D, T)) / fd[:, None], "e2m1")
    return {
        "rows": (n((D, T)) * 0.5 / np.sqrt(D) / ti).astype(np.float32),
        "code0": (np.maximum(n((I, Q)), 0.0)).astype(np.float32),
        "cs1": (np.random.uniform(0.5, 2.0, (I, 1)) * fi[:, None]).astype(np.float32),
        "sig": (n((D, Q)) * 2.0).astype(np.float32),
        "fsc": (np.random.uniform(0.03, 0.06, (D, 1)) * fd[:, None]).astype(np.float32),
        "atom_words": atomp[0],
        "atom_scales": atomp[1],
        "rate": (np.random.uniform(0.3, 1.0, (I, 1))).astype(np.float32),
        "th": (np.random.uniform(0.0, 0.5, (I, 1))).astype(np.float32),
        "offs": striped(idx),
    }


def reference(rows, code0, cs1, sig, fsc, atom_words, atom_scales, rate, th, offs):
    idx = unstriped(offs)
    atomu = unpack_weight(atom_words, atom_scales, "e2m1")
    rt = f64(rows)[:, idx].T
    cw1 = f64(code0) * f64(cs1)
    rtq = mxq(rt, 0, "e4m3")
    cw1q = mxq(cw1, 0, "e4m3")
    r = rtq.T @ cw1q
    e = (f64(sig) - r) * f64(fsc)
    atomidxg = atomu[:, idx]
    eq = mxq(e, 0, "e4m3")
    a = atomidxg.T @ eq
    y = np.maximum(f64(code0) + a * f64(rate) - f64(th), 0.0)
    words, scales = planes(y)
    return y, words, scales

@@ -1,0 +1,195 @@
+from contextlib import ExitStack
+
+import concourse.mybir as mybir
+from concourse.masks import make_identity
+
+D, T, I, Q = 512, 1024, 512, 256
+FLOPS = 2 * 2 * D * I * Q
+
+F32 = mybir.dt.float32
+BF16 = mybir.dt.bfloat16
+I32 = mybir.dt.int32
+U32 = mybir.dt.uint32
+U16 = mybir.dt.uint16
+U8 = mybir.dt.uint8
+FP8X4 = mybir.dt.float8_e4m3fn_x4
+FP4X4 = mybir.dt.float4_e2m1fn_x4
+ALU = mybir.AluOpType
+ACT = mybir.ActivationFunctionType
+
+P = 128
+PACK = 4
+HALVES = 2
+QH = Q // HALVES
+
+
+def tile_attend_pursuitstep_pl_kernel(tc, rows, code0, cs1, sig, fsc, atom_words, atom_scales, rate, th, offs, out_0, out_1, out_2):
+    nc = tc.nc
+    with ExitStack() as ctx:
+        sb = ctx.enter_context(tc.tile_pool(name="sb", bufs=1))
+        late = ctx.enter_context(tc.tile_pool(name="late", bufs=1))
+        ps = ctx.enter_context(tc.psum_pool(name="ps", bufs=1))
+
+        def tile(name, shape, dtype):
+            return sb.tile(shape, dtype, name=name, align_bytes=64)
+
+        offsets = sb.tile([P, I // 16], U16, name="offsets")
+        all_words = tile("all_words", [P, T], U16)
+        all_bytes = tile("all_bytes", [P, T], U8)
+        plane = [tile("plane%d" % j, [P, T], F32) for j in range(PACK - 1)]
+        plane.append(late.tile([P, T], F32, name="plane3", align_bytes=64, offset=0))
+        code = tile("code", [P, PACK, Q], F32)
+        signal = sb.tile([P, PACK, Q], F32, name="signal", tag="signal", align_bytes=64)
+        small = {name: tile(name + "_sb", [P, PACK], F32) for name in ("fsc", "cs1", "th", "rate")}
+
+        def load_small(name, src):
+            nc.sync.dma_start(small[name][:], src.rearrange("(p j) o -> p (j o)", j=PACK))
+
+        rows_by_place = rows.rearrange("(m j) t -> m j t", j=PACK)
+        nc.gpsimd.memset(all_bytes[:].bitcast(I32), 0)
+        warm_in = tile("warm_in", [P, 8], F32)
+        warm_out = tile("warm_out", [P, 8], F32)
+        nc.vector.memset(warm_in[:], 0.0)
+        nc.scalar.activation(warm_out[:], warm_in[:], ACT.Copy)
+        nc.sync.dma_start(offsets[:], offs)
+        nc.sync.dma_start(all_words[:].bitcast(I32), atom_words[0].bitcast(I32))
+        load_small("cs1", cs1)
+        for g in range(4):
+            nc.sync.dma_start(all_bytes[32 * g : 32 * g + 4, :].bitcast(I32), atom_scales[0, 4 * g : 4 * g + 4, :].bitcast(I32))
+        nc.sync.dma_start(code[:], code0.rearrange("(p j) q -> p j q", j=PACK))
+        nc.sync.dma_start(plane[0][:], rows_by_place[:, 0, :])
+        nc.sync.dma_start(plane[1][:], rows_by_place[:, 1, :])
+        load_small("fsc", fsc)
+        nc.sync.dma_start(plane[2][:], rows_by_place[:, 2, :])
+        nc.sync.dma_start(plane[3][:], rows_by_place[:, 3, :])
+        nc.sync.dma_start(signal[:], sig.rearrange("(p j) q -> p j q", j=PACK))
+        load_small("th", th)
+        load_small("rate", rate)
+
+        ident = tile("ident", [P, P], F32)
+        make_identity(nc, ident[:])
+
+        got_words = tile("got_words", [P, I], U16)
+        got_bytes = tile("got_bytes", [P, I], U8)
+        nc.vector.tensor_copy(got_words[:], all_words[:].indirect(offsets[:]))
+        nc.vector.tensor_copy(got_bytes[:], all_bytes[:].indirect(offsets[:]))
+
+        atom_codes = tile("atom_codes", [P, PACK, P], U16)
+        nc.vector.tensor_copy(atom_codes[:], got_words[:].rearrange("p (m j) -> p j m", j=PACK))
+
+        cw_rows = tile("cw_rows", [P, PACK, Q], BF16)
+        for j in range(PACK):
+            nc.scalar.activation(cw_rows[:, j, :], code[:, j, :], ACT.Copy, scale=small["cs1"][:, j : j + 1])
+        cw_in = tile("cw_in", [P, Q, PACK], BF16)
+        nc.vector.tensor_copy(
+            cw_in[:].rearrange("p (c i) t -> p c t i", i=4), cw_rows[:].rearrange("p t (c i) -> p c t i", i=4)
+        )
+
+        got = [tile("got%d" % j, [P, I], BF16) for j in range(PACK)]
+        plane0_bf = tile("plane0_bf", [P, T], BF16)
+        nc.scalar.activation(plane0_bf[:], plane[0][:], ACT.Copy)
+        nc.scalar.activation(got[0][:], plane0_bf[:].indirect(offsets[:]), ACT.Copy)
+        for j in range(1, PACK):
+            nc.vector.tensor_copy(got[j][:], plane[j][:].indirect(offsets[:]))
+
+        cw_codes = tile("cw_codes", [P, Q], U32)
+        cw_plane = tile("cw_plane", [P, Q], U8)
+        nc.vector.quantize_mx(out=cw_codes[:].bitcast(FP8X4), scales=cw_plane[:], in_=cw_in[:].rearrange("p q t -> p (q t)"))
+
+        neg_fsc = tile("neg_fsc", [P, PACK], F32)
+        nc.scalar.activation(neg_fsc[:], small["fsc"][:], ACT.Copy, scale=-1.0)
+        sig_f = tile("sig_f", [P, PACK, Q], F32)
+        for j in range(PACK):
+            nc.scalar.activation(sig_f[:, j, :], signal[:, j, :], ACT.Copy, scale=small["fsc"][:, j : j + 1])
+
+        e_rows = tile("e_rows", [P, HALVES, PACK, QH], BF16)
+        for j in range(PACK):
+            turned = ps.tile([P, 2, P], F32, name="turned", tag="turned", bufs=3)
+            words = got[j][:].bitcast(F32)
+            for u in range(2):
+                nc.tensor.transpose(turned[:, u, :], words[:, u : I // 2 : 2], ident[:])
+            rt_in = sb.tile([P, P * PACK], BF16, name="rt_in%d" % j, align_bytes=64)
+            copy_out = nc.scalar.copy if j < PACK - 1 else nc.vector.tensor_copy
+            copy_out(rt_in[:].bitcast(F32).rearrange("p (m u) -> p m u", u=2), turned[:].rearrange("p u m -> p m u"))
+            rt_codes = late.tile([P, P], U32, name="rt_codes%d" % j, align_bytes=64, offset=512 * j)
+            rt_plane = tile("rt_plane%d" % j, [P, P], U8)
+            nc.vector.quantize_mx(out=rt_codes[:].bitcast(FP8X4), scales=rt_plane[:], in_=rt_in[:])
+            if j < PACK - 1:
+                r = ps.tile([P, Q], F32, name="r%d" % j, tag="bank%d" % j)
+                nc.tensor.matmul_mx(
+                    out=r[:], lhsT=rt_codes[:].bitcast(FP8X4), lhsT_scale=rt_plane[:],
+                    rhs=cw_codes[:].bitcast(FP8X4), rhs_scale=cw_plane[:], start=True, stop=True,
+                )
+                nc.vector.scalar_tensor_tensor(
+                    e_rows[:, :, j, :], r[:].rearrange("p (h q) -> p h q", h=HALVES), neg_fsc[:, j : j + 1],
+                    sig_f[:, j, :].rearrange("p (h q) -> p h q", h=HALVES), ALU.mult, ALU.add,
+                )
+            else:
+                for h in range(HALVES):
+                    cols = slice(h * QH, (h + 1) * QH)
+                    r = ps.tile([P, QH], F32, name="r%d_%d" % (j, h), tag="bank%d" % (j + h))
+                    nc.tensor.matmul_mx(
+                        out=r[:], lhsT=rt_codes[:].bitcast(FP8X4), lhsT_scale=rt_plane[:],
+                        rhs=cw_codes[:, cols].bitcast(FP8X4), rhs_scale=cw_plane[:, cols], start=True, stop=True,
+                    )
+                    nc.vector.scalar_tensor_tensor(
+                        e_rows[:, h, j, :], r[:], neg_fsc[:, j : j + 1], sig_f[:, j, cols], ALU.mult, ALU.add
+                    )
+
+        atom_plane = late.tile([P, PACK, P], U8, name="atom_plane", align_bytes=64, offset=3072)
+        nc.vector.tensor_copy(atom_plane[:], got_bytes[:].rearrange("p (m j) -> p j m", j=PACK))
+        th_less_code = tile("th_less_code", [P, PACK, Q], F32)
+        for j in range(PACK):
+            nc.scalar.activation(th_less_code[:, j, :], code[:, j, :], ACT.Identity, bias=small["th"][:, j : j + 1], scale=-1.0)
+
+        y_codes = tile("y_codes", [P, Q], U32)
+        y_plane = tile("y_plane", [P, Q], U8)
+        out_rows = out_0.rearrange("(p j) q -> p j q", j=PACK)
+        out_words = out_1[0].rearrange("p c r -> p (c r)").bitcast(I32)
+        e_in, e_codes, e_plane, z, y_in = [], [], [], [], []
+        for h in range(HALVES):
+            e_in.append(tile("e_in%d" % h, [P, QH, PACK], BF16))
+            nc.vector.tensor_copy(
+                e_in[h][:].rearrange("p (c i) t -> p c t i", i=4), e_rows[:, h].rearrange("p t (c i) -> p c t i", i=4)
+            )
+        for h in range(HALVES):
+            e_codes.append(tile("e_codes%d" % h, [P, QH], U32))
+            e_plane.append(tile("e_plane%d" % h, [P, QH], U8))
+            nc.vector.quantize_mx(out=e_codes[h][:].bitcast(FP8X4), scales=e_plane[h][:], in_=e_in[h][:].rearrange("p q t -> p (q t)"))
+        for h in range(HALVES):
+            cols = slice(h * QH, (h + 1) * QH)
+            z.append(tile("z%d" % h, [P, PACK, QH], F32))
+            for pair in range(2):
+                score = ps.tile([P, 2, QH], F32, name="score%d_%d" % (h, pair), tag="bank%d" % (2 * h + pair))
+                for k in range(2):
+                    j = 2 * pair + k
+                    nc.tensor.matmul_mx(
+                        out=score[:, k, :], lhsT=atom_codes[:, j, :].bitcast(FP4X4), lhsT_scale=atom_plane[:, j, :],
+                        rhs=e_codes[h][:].bitcast(FP8X4), rhs_scale=e_plane[h][:], start=True, stop=True,
+                    )
+                for k in range(2):
+                    j = 2 * pair + k
+                    nc.vector.scalar_tensor_tensor(
+                        z[h][:, j, :], score[:, k, :], small["rate"][:, j : j + 1], th_less_code[:, j, cols], ALU.mult, ALU.subtract
+                    )
+        for h in range(HALVES):
+            y_in.append(tile("y_in%d" % h, [P, QH, PACK], BF16))
+            grouped = y_in[h][:].rearrange("p (c i) t -> p c t i", i=4)
+            by_rows = z[h][:].rearrange("p t (c i) -> p c t i", i=4)
+            if h == 0:
+                nc.scalar.activation(grouped, by_rows, ACT.Relu)
+            else:
+                nc.vector.tensor_scalar(grouped, by_rows, 0.0, None, ALU.max)
+        for h in range(HALVES):
+            cols = slice(h * QH, (h + 1) * QH)
+            y = tile("y%d" % h, [P, PACK, QH], F32)
+            if h == 0:
+                nc.scalar.activation(y[:], z[h][:], ACT.Relu)
+            else:
+                nc.vector.tensor_scalar(y[:], z[h][:], 0.0, None, ALU.max)
+            nc.sync.dma_start(out_rows[:, :, cols], y[:])
+            nc.vector.quantize_mx(out=y_codes[:, cols].bitcast(FP8X4), scales=y_plane[:, cols], in_=y_in[h][:].rearrange("p q t -> p (q t)"))
+            nc.sync.dma_start(out_words[:, cols], y_codes[:, cols].bitcast(I32))
+        for g in range(4):
+            queue = nc.sync if g % 2 else nc.scalar
+            queue.dma_start(out_2[0, 4 * g : 4 * g + 4, :].bitcast(I32), y_plane[32 * g : 32 * g + 4, :].bitcast(I32))

@@ -40,7 +40,8 @@ def tile_attend_pursuitstep_pl_kernel(tc, rows, code0, cs1, sig, fsc, atom_words
         plane.append(late.tile([P, T], F32, name="plane3", align_bytes=64, offset=0))
         code = tile("code", [P, PACK, Q], F32)
         signal = sb.tile([P, PACK, Q], F32, name="signal", tag="signal", align_bytes=64)
-        small = {name: tile(name + "_sb", [P, PACK], F32) for name in ("fsc", "cs1", "th", "rate")}
+        small = {name: tile(name + "_sb", [P, PACK], F32) for name in ("fsc", "th", "rate")}
+        cs1_wide = late.tile([P, 256], F32, name="cs1_wide", align_bytes=64, offset=6144)
 
         def load_small(name, src):
             nc.sync.dma_start(small[name][:], src.rearrange("(p j) o -> p (j o)", j=PACK))
@@ -51,17 +52,17 @@ def tile_attend_pursuitstep_pl_kernel(tc, rows, code0, cs1, sig, fsc, atom_words
         warm_out = tile("warm_out", [P, 8], F32)
         nc.vector.memset(warm_in[:], 0.0)
         nc.scalar.activation(warm_out[:], warm_in[:], ACT.Copy)
-        nc.sync.dma_start(offsets[:], offs)
         nc.sync.dma_start(all_words[:].bitcast(I32), atom_words[0].bitcast(I32))
-        load_small("cs1", cs1)
+        nc.sync.dma_start(offsets[:], offs)
+        nc.sync.dma_start(plane[0][:], rows_by_place[:, 0, :])
         for g in range(4):
             nc.sync.dma_start(all_bytes[32 * g : 32 * g + 4, :].bitcast(I32), atom_scales[0, 4 * g : 4 * g + 4, :].bitcast(I32))
-        nc.sync.dma_start(code[:], code0.rearrange("(p j) q -> p j q", j=PACK))
-        nc.sync.dma_start(plane[0][:], rows_by_place[:, 0, :])
         nc.sync.dma_start(plane[1][:], rows_by_place[:, 1, :])
-        load_small("fsc", fsc)
         nc.sync.dma_start(plane[2][:], rows_by_place[:, 2, :])
         nc.sync.dma_start(plane[3][:], rows_by_place[:, 3, :])
+        nc.sync.dma_start(cs1_wide[:, :PACK], cs1.rearrange("(p j) o -> p (j o)", j=PACK))
+        nc.sync.dma_start(code[:], code0.rearrange("(p j) q -> p j q", j=PACK))
+        load_small("fsc", fsc)
         nc.sync.dma_start(signal[:], sig.rearrange("(p j) q -> p j q", j=PACK))
         load_small("th", th)
         load_small("rate", rate)
@@ -72,35 +73,34 @@ def tile_attend_pursuitstep_pl_kernel(tc, rows, code0, cs1, sig, fsc, atom_words
         got_words = tile("got_words", [P, I], U16)
         got_bytes = tile("got_bytes", [P, I], U8)
         nc.vector.tensor_copy(got_words[:], all_words[:].indirect(offsets[:]))
-        nc.vector.tensor_copy(got_bytes[:], all_bytes[:].indirect(offsets[:]))
-
         atom_codes = tile("atom_codes", [P, PACK, P], U16)
         nc.vector.tensor_copy(atom_codes[:], got_words[:].rearrange("p (m j) -> p j m", j=PACK))
-
-        cw_rows = tile("cw_rows", [P, PACK, Q], BF16)
-        for j in range(PACK):
-            nc.scalar.activation(cw_rows[:, j, :], code[:, j, :], ACT.Copy, scale=small["cs1"][:, j : j + 1])
-        cw_in = tile("cw_in", [P, Q, PACK], BF16)
-        nc.vector.tensor_copy(
-            cw_in[:].rearrange("p (c i) t -> p c t i", i=4), cw_rows[:].rearrange("p t (c i) -> p c t i", i=4)
-        )
+        nc.vector.tensor_copy(got_bytes[:], all_bytes[:].indirect(offsets[:]))
 
         got = [tile("got%d" % j, [P, I], BF16) for j in range(PACK)]
-        plane0_bf = tile("plane0_bf", [P, T], BF16)
-        nc.scalar.activation(plane0_bf[:], plane[0][:], ACT.Copy)
-        nc.scalar.activation(got[0][:], plane0_bf[:].indirect(offsets[:]), ACT.Copy)
-        for j in range(1, PACK):
-            nc.vector.tensor_copy(got[j][:], plane[j][:].indirect(offsets[:]))
+        narrow = [tile("narrow0", [P, T], BF16), late.tile([P, T], BF16, name="narrow1", align_bytes=64, offset=4096)]
+        nc.scalar.activation(narrow[0][:], plane[0][:], ACT.Copy)
+        nc.vector.tensor_copy(narrow[1][:], plane[1][:])
+        for j in range(PACK):
+            if j < 2:
+                nc.scalar.activation(got[j][:], narrow[j][:].indirect(offsets[:]), ACT.Copy)
+            else:
+                nc.vector.tensor_copy(got[j][:], plane[j][:].indirect(offsets[:]))
 
-        cw_codes = tile("cw_codes", [P, Q], U32)
+        cw_in = tile("cw_in", [P, Q, PACK], BF16)
+        nc.vector.tensor_tensor(
+            cw_in[:].rearrange("p (c i) t -> p c t i", i=4),
+            code[:].rearrange("p t (c i) -> p c t i", i=4),
+            cs1_wide[:, :PACK].unsqueeze(1).unsqueeze(3).to_broadcast([P, Q // 4, PACK, 4]),
+            ALU.mult,
+        )
+        cw_codes = late.tile([P, Q], U32, name="cw_codes", align_bytes=64, offset=2048)
         cw_plane = tile("cw_plane", [P, Q], U8)
         nc.vector.quantize_mx(out=cw_codes[:].bitcast(FP8X4), scales=cw_plane[:], in_=cw_in[:].rearrange("p q t -> p (q t)"))
 
         neg_fsc = tile("neg_fsc", [P, PACK], F32)
         nc.scalar.activation(neg_fsc[:], small["fsc"][:], ACT.Copy, scale=-1.0)
         sig_f = tile("sig_f", [P, PACK, Q], F32)
-        for j in range(PACK):
-            nc.scalar.activation(sig_f[:, j, :], signal[:, j, :], ACT.Copy, scale=small["fsc"][:, j : j + 1])
 
         e_rows = tile("e_rows", [P, HALVES, PACK, QH], BF16)
         for j in range(PACK):
@@ -108,11 +108,14 @@ def tile_attend_pursuitstep_pl_kernel(tc, rows, code0, cs1, sig, fsc, atom_words
             words = got[j][:].bitcast(F32)
             for u in range(2):
                 nc.tensor.transpose(turned[:, u, :], words[:, u : I // 2 : 2], ident[:])
-            rt_in = sb.tile([P, P * PACK], BF16, name="rt_in%d" % j, align_bytes=64)
-            copy_out = nc.scalar.copy if j < PACK - 1 else nc.vector.tensor_copy
-            copy_out(rt_in[:].bitcast(F32).rearrange("p (m u) -> p m u", u=2), turned[:].rearrange("p u m -> p m u"))
+            if j == 0:
+                rt_in = late.tile([P, P * PACK], BF16, name="rt_in0", align_bytes=64, offset=4096)
+            else:
+                rt_in = tile("rt_in%d" % j, [P, P * PACK], BF16)
+            nc.scalar.copy(rt_in[:].bitcast(F32).rearrange("p (m u) -> p m u", u=2), turned[:].rearrange("p u m -> p m u"))
+            nc.scalar.activation(sig_f[:, j, :], signal[:, j, :], ACT.Copy, scale=small["fsc"][:, j : j + 1])
             rt_codes = late.tile([P, P], U32, name="rt_codes%d" % j, align_bytes=64, offset=512 * j)
-            rt_plane = tile("rt_plane%d" % j, [P, P], U8)
+            rt_plane = late.tile([P, P], U8, name="rt_plane%d" % j, align_bytes=64, offset=6144 + P * j)
             nc.vector.quantize_mx(out=rt_codes[:].bitcast(FP8X4), scales=rt_plane[:], in_=rt_in[:])
             if j < PACK - 1:
                 r = ps.tile([P, Q], F32, name="r%d" % j, tag="bank%d" % j)
@@ -136,7 +139,7 @@ def tile_attend_pursuitstep_pl_kernel(tc, rows, code0, cs1, sig, fsc, atom_words
                         e_rows[:, h, j, :], r[:], neg_fsc[:, j : j + 1], sig_f[:, j, cols], ALU.mult, ALU.add
                     )
 
-        atom_plane = late.tile([P, PACK, P], U8, name="atom_plane", align_bytes=64, offset=3072)
+        atom_plane = late.tile([P, PACK, P], U8, name="atom_plane", align_bytes=64, offset=6144 + 512)
         nc.vector.tensor_copy(atom_plane[:], got_bytes[:].rearrange("p (m j) -> p j m", j=PACK))
         th_less_code = tile("th_less_code", [P, PACK, Q], F32)
         for j in range(PACK):
@@ -146,10 +149,11 @@ def tile_attend_pursuitstep_pl_kernel(tc, rows, code0, cs1, sig, fsc, atom_words
         y_plane = tile("y_plane", [P, Q], U8)
         out_rows = out_0.rearrange("(p j) q -> p j q", j=PACK)
         out_words = out_1[0].rearrange("p c r -> p (c r)").bitcast(I32)
-        e_in, e_codes, e_plane, z, y_in = [], [], [], [], []
+        e_in, e_codes, e_plane, z = [], [], [], []
         for h in range(HALVES):
             e_in.append(tile("e_in%d" % h, [P, QH, PACK], BF16))
-            nc.vector.tensor_copy(
+            regroup = nc.vector.tensor_copy if h == 0 else nc.scalar.copy
+            regroup(
                 e_in[h][:].rearrange("p (c i) t -> p c t i", i=4), e_rows[:, h].rearrange("p t (c i) -> p c t i", i=4)
             )
         for h in range(HALVES):
@@ -172,24 +176,21 @@ def tile_attend_pursuitstep_pl_kernel(tc, rows, code0, cs1, sig, fsc, atom_words
                     nc.vector.scalar_tensor_tensor(
                         z[h][:, j, :], score[:, k, :], small["rate"][:, j : j + 1], th_less_code[:, j, cols], ALU.mult, ALU.subtract
                     )
-        for h in range(HALVES):
-            y_in.append(tile("y_in%d" % h, [P, QH, PACK], BF16))
-            grouped = y_in[h][:].rearrange("p (c i) t -> p c t i", i=4)
-            by_rows = z[h][:].rearrange("p t (c i) -> p c t i", i=4)
-            if h == 0:
-                nc.scalar.activation(grouped, by_rows, ACT.Relu)
-            else:
-                nc.vector.tensor_scalar(grouped, by_rows, 0.0, None, ALU.max)
+        y_in = tile("y_in", [P, Q, PACK], BF16)
         for h in range(HALVES):
             cols = slice(h * QH, (h + 1) * QH)
             y = tile("y%d" % h, [P, PACK, QH], F32)
+            grouped = y_in[:, cols, :].rearrange("p (c i) t -> p c t i", i=4)
+            by_rows = z[h][:].rearrange("p t (c i) -> p c t i", i=4)
             if h == 0:
                 nc.scalar.activation(y[:], z[h][:], ACT.Relu)
+                nc.scalar.activation(grouped, by_rows, ACT.Relu)
             else:
+                nc.vector.tensor_scalar(grouped, by_rows, 0.0, None, ALU.max)
                 nc.vector.tensor_scalar(y[:], z[h][:], 0.0, None, ALU.max)
             nc.sync.dma_start(out_rows[:, :, cols], y[:])
-            nc.vector.quantize_mx(out=y_codes[:, cols].bitcast(FP8X4), scales=y_plane[:, cols], in_=y_in[h][:].rearrange("p q t -> p (q t)"))
-            nc.sync.dma_start(out_words[:, cols], y_codes[:, cols].bitcast(I32))
+        nc.vector.quantize_mx(out=y_codes[:].bitcast(FP8X4), scales=y_plane[:], in_=y_in[:].rearrange("p q t -> p (q t)"))
+        nc.sync.dma_start(out_words, y_codes[:].bitcast(I32))
         for g in range(4):
             queue = nc.sync if g % 2 else nc.scalar
             queue.dma_start(out_2[0, 4 * g : 4 * g + 4, :].bitcast(I32), y_plane[32 * g : 32 * g + 4, :].bitcast(I32))

@@ -48,10 +48,7 @@ def tile_attend_pursuitstep_pl_kernel(tc, rows, code0, cs1, sig, fsc, atom_words
 
         rows_by_place = rows.rearrange("(m j) t -> m j t", j=PACK)
         nc.gpsimd.memset(all_bytes[:].bitcast(I32), 0)
-        warm_in = tile("warm_in", [P, 8], F32)
-        warm_out = tile("warm_out", [P, 8], F32)
-        nc.vector.memset(warm_in[:], 0.0)
-        nc.scalar.activation(warm_out[:], warm_in[:], ACT.Copy)
+        nc.scalar.dma_start(small["fsc"][:], fsc.rearrange("(p j) o -> p (j o)", j=PACK))
         nc.sync.dma_start(all_words[:].bitcast(I32), atom_words[0].bitcast(I32))
         nc.sync.dma_start(offsets[:], offs)
         nc.sync.dma_start(plane[0][:], rows_by_place[:, 0, :])
@@ -62,7 +59,6 @@ def tile_attend_pursuitstep_pl_kernel(tc, rows, code0, cs1, sig, fsc, atom_words
         nc.sync.dma_start(plane[3][:], rows_by_place[:, 3, :])
         nc.sync.dma_start(cs1_wide[:, :PACK], cs1.rearrange("(p j) o -> p (j o)", j=PACK))
         nc.sync.dma_start(code[:], code0.rearrange("(p j) q -> p j q", j=PACK))
-        load_small("fsc", fsc)
         nc.sync.dma_start(signal[:], sig.rearrange("(p j) q -> p j q", j=PACK))
         load_small("th", th)
         load_small("rate", rate)

@@ -73,12 +73,14 @@ def tile_attend_pursuitstep_pl_kernel(tc, rows, code0, cs1, sig, fsc, atom_words
         nc.vector.tensor_copy(atom_codes[:], got_words[:].rearrange("p (m j) -> p j m", j=PACK))
         nc.vector.tensor_copy(got_bytes[:], all_bytes[:].indirect(offsets[:]))
 
+        atom_plane = tile("atom_plane", [P, PACK, P], U8)
+        nc.vector.tensor_copy(atom_plane[:], got_bytes[:].rearrange("p (m j) -> p j m", j=PACK))
+
         got = [tile("got%d" % j, [P, I], BF16) for j in range(PACK)]
         narrow = [tile("narrow0", [P, T], BF16), late.tile([P, T], BF16, name="narrow1", align_bytes=64, offset=4096)]
-        nc.scalar.activation(narrow[0][:], plane[0][:], ACT.Copy)
-        nc.vector.tensor_copy(narrow[1][:], plane[1][:])
         for j in range(PACK):
             if j < 2:
+                nc.scalar.activation(narrow[j][:], plane[j][:], ACT.Copy)
                 nc.scalar.activation(got[j][:], narrow[j][:].indirect(offsets[:]), ACT.Copy)
             else:
                 nc.vector.tensor_copy(got[j][:], plane[j][:].indirect(offsets[:]))
@@ -135,8 +137,6 @@ def tile_attend_pursuitstep_pl_kernel(tc, rows, code0, cs1, sig, fsc, atom_words
                         e_rows[:, h, j, :], r[:], neg_fsc[:, j : j + 1], sig_f[:, j, cols], ALU.mult, ALU.add
                     )
 
-        atom_plane = late.tile([P, PACK, P], U8, name="atom_plane", align_bytes=64, offset=6144 + 512)
-        nc.vector.tensor_copy(atom_plane[:], got_bytes[:].rearrange("p (m j) -> p j m", j=PACK))
         th_less_code = tile("th_less_code", [P, PACK, Q], F32)
         for j in range(PACK):
             nc.scalar.activation(th_less_code[:, j, :], code[:, j, :], ACT.Identity, bias=small["th"][:, j : j + 1], scale=-1.0)
@@ -176,16 +176,14 @@ def tile_attend_pursuitstep_pl_kernel(tc, rows, code0, cs1, sig, fsc, atom_words
         for h in range(HALVES):
             cols = slice(h * QH, (h + 1) * QH)
             y = tile("y%d" % h, [P, PACK, QH], F32)
-            grouped = y_in[:, cols, :].rearrange("p (c i) t -> p c t i", i=4)
-            by_rows = z[h][:].rearrange("p t (c i) -> p c t i", i=4)
-            if h == 0:
-                nc.scalar.activation(y[:], z[h][:], ACT.Relu)
-                nc.scalar.activation(grouped, by_rows, ACT.Relu)
-            else:
-                nc.vector.tensor_scalar(grouped, by_rows, 0.0, None, ALU.max)
-                nc.vector.tensor_scalar(y[:], z[h][:], 0.0, None, ALU.max)
+            nc.scalar.activation(y[:], z[h][:], ACT.Relu)
             nc.sync.dma_start(out_rows[:, :, cols], y[:])
-        nc.vector.quantize_mx(out=y_codes[:].bitcast(FP8X4), scales=y_plane[:], in_=y_in[:].rearrange("p q t -> p (q t)"))
+            nc.vector.tensor_scalar(
+                y_in[:, cols, :].rearrange("p (c i) t -> p c t i", i=4), z[h][:].rearrange("p t (c i) -> p c t i", i=4), 0.0, None, ALU.max
+            )
+        for h in range(HALVES):
+            cols = slice(h * QH, (h + 1) * QH)
+            nc.vector.quantize_mx(out=y_codes[:, cols].bitcast(FP8X4), scales=y_plane[:, cols], in_=y_in[:, cols, :].rearrange("p q t -> p (q t)"))
         nc.sync.dma_start(out_words, y_codes[:].bitcast(I32))
         for g in range(4):
             queue = nc.sync if g % 2 else nc.scalar

from contextlib import ExitStack

import concourse.mybir as mybir
from concourse.masks import make_identity

D, T, I, Q = 512, 1024, 512, 256
FLOPS = 2 * 2 * D * I * Q

F32 = mybir.dt.float32
BF16 = mybir.dt.bfloat16
I32 = mybir.dt.int32
U32 = mybir.dt.uint32
U16 = mybir.dt.uint16
U8 = mybir.dt.uint8
FP8X4 = mybir.dt.float8_e4m3fn_x4
FP4X4 = mybir.dt.float4_e2m1fn_x4
ALU = mybir.AluOpType
ACT = mybir.ActivationFunctionType

P = 128
PACK = 4
HALVES = 2
QH = Q // HALVES


def tile_attend_pursuitstep_pl_kernel(tc, rows, code0, cs1, sig, fsc, atom_words, atom_scales, rate, th, offs, out_0, out_1, out_2):
    nc = tc.nc
    with ExitStack() as ctx:
        sb = ctx.enter_context(tc.tile_pool(name="sb", bufs=1))
        late = ctx.enter_context(tc.tile_pool(name="late", bufs=1))
        ps = ctx.enter_context(tc.psum_pool(name="ps", bufs=1))

        def tile(name, shape, dtype):
            return sb.tile(shape, dtype, name=name, align_bytes=64)

        offsets = sb.tile([P, I // 16], U16, name="offsets")
        all_words = tile("all_words", [P, T], U16)
        all_bytes = tile("all_bytes", [P, T], U8)
        plane = [tile("plane%d" % j, [P, T], F32) for j in range(PACK - 1)]
        plane.append(late.tile([P, T], F32, name="plane3", align_bytes=64, offset=0))
        code = tile("code", [P, PACK, Q], F32)
        signal = sb.tile([P, PACK, Q], F32, name="signal", tag="signal", align_bytes=64)
        small = {name: tile(name + "_sb", [P, PACK], F32) for name in ("fsc", "th", "rate")}
        cs1_wide = late.tile([P, 256], F32, name="cs1_wide", align_bytes=64, offset=6144)

        def load_small(name, src):
            nc.sync.dma_start(small[name][:], src.rearrange("(p j) o -> p (j o)", j=PACK))

        rows_by_place = rows.rearrange("(m j) t -> m j t", j=PACK)
        nc.gpsimd.memset(all_bytes[:].bitcast(I32), 0)
        nc.scalar.dma_start(small["fsc"][:], fsc.rearrange("(p j) o -> p (j o)", j=PACK))
        nc.sync.dma_start(all_words[:].bitcast(I32), atom_words[0].bitcast(I32))
        nc.sync.dma_start(offsets[:], offs)
        nc.sync.dma_start(plane[0][:], rows_by_place[:, 0, :])
        for g in range(4):
            nc.sync.dma_start(all_bytes[32 * g : 32 * g + 4, :].bitcast(I32), atom_scales[0, 4 * g : 4 * g + 4, :].bitcast(I32))
        nc.sync.dma_start(plane[1][:], rows_by_place[:, 1, :])
        nc.sync.dma_start(plane[2][:], rows_by_place[:, 2, :])
        nc.sync.dma_start(plane[3][:], rows_by_place[:, 3, :])
        nc.sync.dma_start(cs1_wide[:, :PACK], cs1.rearrange("(p j) o -> p (j o)", j=PACK))
        nc.sync.dma_start(code[:], code0.rearrange("(p j) q -> p j q", j=PACK))
        nc.sync.dma_start(signal[:], sig.rearrange("(p j) q -> p j q", j=PACK))
        load_small("th", th)
        load_small("rate", rate)

        ident = tile("ident", [P, P], F32)
        make_identity(nc, ident[:])

        got_words = tile("got_words", [P, I], U16)
        got_bytes = tile("got_bytes", [P, I], U8)
        nc.vector.tensor_copy(got_words[:], all_words[:].indirect(offsets[:]))
        atom_codes = tile("atom_codes", [P, PACK, P], U16)
        nc.vector.tensor_copy(atom_codes[:], got_words[:].rearrange("p (m j) -> p j m", j=PACK))
        nc.vector.tensor_copy(got_bytes[:], all_bytes[:].indirect(offsets[:]))

        atom_plane = tile("atom_plane", [P, PACK, P], U8)
        nc.vector.tensor_copy(atom_plane[:], got_bytes[:].rearrange("p (m j) -> p j m", j=PACK))

        got = [tile("got%d" % j, [P, I], BF16) for j in range(PACK)]
        narrow = [tile("narrow0", [P, T], BF16), late.tile([P, T], BF16, name="narrow1", align_bytes=64, offset=4096)]
        for j in range(PACK):
            if j < 2:
                nc.scalar.activation(narrow[j][:], plane[j][:], ACT.Copy)
                nc.scalar.activation(got[j][:], narrow[j][:].indirect(offsets[:]), ACT.Copy)
            else:
                nc.vector.tensor_copy(got[j][:], plane[j][:].indirect(offsets[:]))

        cw_in = tile("cw_in", [P, Q, PACK], BF16)
        nc.vector.tensor_tensor(
            cw_in[:].rearrange("p (c i) t -> p c t i", i=4),
            code[:].rearrange("p t (c i) -> p c t i", i=4),
            cs1_wide[:, :PACK].unsqueeze(1).unsqueeze(3).to_broadcast([P, Q // 4, PACK, 4]),
            ALU.mult,
        )
        cw_codes = late.tile([P, Q], U32, name="cw_codes", align_bytes=64, offset=2048)
        cw_plane = tile("cw_plane", [P, Q], U8)
        nc.vector.quantize_mx(out=cw_codes[:].bitcast(FP8X4), scales=cw_plane[:], in_=cw_in[:].rearrange("p q t -> p (q t)"))

        neg_fsc = tile("neg_fsc", [P, PACK], F32)
        nc.scalar.activation(neg_fsc[:], small["fsc"][:], ACT.Copy, scale=-1.0)
        sig_f = tile("sig_f", [P, PACK, Q], F32)

        e_rows = tile("e_rows", [P, HALVES, PACK, QH], BF16)
        for j in range(PACK):
            turned = ps.tile([P, 2, P], F32, name="turned", tag="turned", bufs=3)
            words = got[j][:].bitcast(F32)
            for u in range(2):
                nc.tensor.transpose(turned[:, u, :], words[:, u : I // 2 : 2], ident[:])
            if j == 0:
                rt_in = late.tile([P, P * PACK], BF16, name="rt_in0", align_bytes=64, offset=4096)
            else:
                rt_in = tile("rt_in%d" % j, [P, P * PACK], BF16)
            nc.scalar.copy(rt_in[:].bitcast(F32).rearrange("p (m u) -> p m u", u=2), turned[:].rearrange("p u m -> p m u"))
            nc.scalar.activation(sig_f[:, j, :], signal[:, j, :], ACT.Copy, scale=small["fsc"][:, j : j + 1])
            rt_codes = late.tile([P, P], U32, name="rt_codes%d" % j, align_bytes=64, offset=512 * j)
            rt_plane = late.tile([P, P], U8, name="rt_plane%d" % j, align_bytes=64, offset=6144 + P * j)
            nc.vector.quantize_mx(out=rt_codes[:].bitcast(FP8X4), scales=rt_plane[:], in_=rt_in[:])
            if j < PACK - 1:
                r = ps.tile([P, Q], F32, name="r%d" % j, tag="bank%d" % j)
                nc.tensor.matmul_mx(
                    out=r[:], lhsT=rt_codes[:].bitcast(FP8X4), lhsT_scale=rt_plane[:],
                    rhs=cw_codes[:].bitcast(FP8X4), rhs_scale=cw_plane[:], start=True, stop=True,
                )
                nc.vector.scalar_tensor_tensor(
                    e_rows[:, :, j, :], r[:].rearrange("p (h q) -> p h q", h=HALVES), neg_fsc[:, j : j + 1],
                    sig_f[:, j, :].rearrange("p (h q) -> p h q", h=HALVES), ALU.mult, ALU.add,
                )
            else:
                for h in range(HALVES):
                    cols = slice(h * QH, (h + 1) * QH)
                    r = ps.tile([P, QH], F32, name="r%d_%d" % (j, h), tag="bank%d" % (j + h))
                    nc.tensor.matmul_mx(
                        out=r[:], lhsT=rt_codes[:].bitcast(FP8X4), lhsT_scale=rt_plane[:],
                        rhs=cw_codes[:, cols].bitcast(FP8X4), rhs_scale=cw_plane[:, cols], start=True, stop=True,
                    )
                    nc.vector.scalar_tensor_tensor(
                        e_rows[:, h, j, :], r[:], neg_fsc[:, j : j + 1], sig_f[:, j, cols], ALU.mult, ALU.add
                    )

        th_less_code = tile("th_less_code", [P, PACK, Q], F32)
        for j in range(PACK):
            nc.scalar.activation(th_less_code[:, j, :], code[:, j, :], ACT.Identity, bias=small["th"][:, j : j + 1], scale=-1.0)

        y_codes = tile("y_codes", [P, Q], U32)
        y_plane = tile("y_plane", [P, Q], U8)
        out_rows = out_0.rearrange("(p j) q -> p j q", j=PACK)
        out_words = out_1[0].rearrange("p c r -> p (c r)").bitcast(I32)
        e_in, e_codes, e_plane, z = [], [], [], []
        for h in range(HALVES):
            e_in.append(tile("e_in%d" % h, [P, QH, PACK], BF16))
            regroup = nc.vector.tensor_copy if h == 0 else nc.scalar.copy
            regroup(
                e_in[h][:].rearrange("p (c i) t -> p c t i", i=4), e_rows[:, h].rearrange("p t (c i) -> p c t i", i=4)
            )
        for h in range(HALVES):
            e_codes.append(tile("e_codes%d" % h, [P, QH], U32))
            e_plane.append(tile("e_plane%d" % h, [P, QH], U8))
            nc.vector.quantize_mx(out=e_codes[h][:].bitcast(FP8X4), scales=e_plane[h][:], in_=e_in[h][:].rearrange("p q t -> p (q t)"))
        for h in range(HALVES):
            cols = slice(h * QH, (h + 1) * QH)
            z.append(tile("z%d" % h, [P, PACK, QH], F32))
            for pair in range(2):
                score = ps.tile([P, 2, QH], F32, name="score%d_%d" % (h, pair), tag="bank%d" % (2 * h + pair))
                for k in range(2):
                    j = 2 * pair + k
                    nc.tensor.matmul_mx(
                        out=score[:, k, :], lhsT=atom_codes[:, j, :].bitcast(FP4X4), lhsT_scale=atom_plane[:, j, :],
                        rhs=e_codes[h][:].bitcast(FP8X4), rhs_scale=e_plane[h][:], start=True, stop=True,
                    )
                for k in range(2):
                    j = 2 * pair + k
                    nc.vector.scalar_tensor_tensor(
                        z[h][:, j, :], score[:, k, :], small["rate"][:, j : j + 1], th_less_code[:, j, cols], ALU.mult, ALU.subtract
                    )
        y_in = tile("y_in", [P, Q, PACK], BF16)
        for h in range(HALVES):
            cols = slice(h * QH, (h + 1) * QH)
            y = tile("y%d" % h, [P, PACK, QH], F32)
            nc.scalar.activation(y[:], z[h][:], ACT.Relu)
            nc.sync.dma_start(out_rows[:, :, cols], y[:])
            nc.vector.tensor_scalar(
                y_in[:, cols, :].rearrange("p (c i) t -> p c t i", i=4), z[h][:].rearrange("p t (c i) -> p c t i", i=4), 0.0, None, ALU.max
            )
        for h in range(HALVES):
            cols = slice(h * QH, (h + 1) * QH)
            nc.vector.quantize_mx(out=y_codes[:, cols].bitcast(FP8X4), scales=y_plane[:, cols], in_=y_in[:, cols, :].rearrange("p q t -> p (q t)"))
        nc.sync.dma_start(out_words, y_codes[:].bitcast(I32))
        for g in range(4):
            queue = nc.sync if g % 2 else nc.scalar
            queue.dma_start(out_2[0, 4 * g : 4 * g + 4, :].bitcast(I32), y_plane[32 * g : 32 * g + 4, :].bitcast(I32))
